import numpy as np
import ml_dtypes


def mxq(x, axis, fmt="e4m3"):
    dtype, down = {"e4m3": (ml_dtypes.float8_e4m3fn, 7), "e5m2": (ml_dtypes.float8_e5m2, 14)}[fmt]
    v = np.moveaxis(np.asarray(x, np.float32).astype(ml_dtypes.bfloat16).astype(np.float64), axis, -1)
    blocks = v.reshape(v.shape[:-1] + (-1, 32))
    amax = np.abs(blocks).max(-1, keepdims=True)
    byte = np.maximum(np.where(amax > 0, np.frexp(amax)[1] - 1 + 127, 0) - down, 1)
    scale = np.exp2(byte - 127.0)
    codes = (blocks / scale).astype(np.float32).astype(dtype).astype(np.float64)
    return np.moveaxis((codes * scale).reshape(v.shape), -1, axis)


WIDE = False


def mx_kscale(k):
    if not WIDE:
        return np.ones(k)
    levels = np.array([10, -10, 5, -5, 0])
    if k % 512:
        return np.exp2(np.random.permutation(np.resize(levels, k // 32))).repeat(32)
    a = np.empty((k // 512, 16))
    for p in range(k // 512):
        a[p, :8] = np.random.permutation(np.resize(levels, 8))
        for g in range(8):
            far = levels[np.abs(levels - a[p, g]) >= 10]
            a[p, g + 8] = far[np.random.randint(len(far))]
    return np.exp2(a.ravel()).repeat(32)


def f64(x):
    return np.asarray(x).astype(np.float64)


def striped(idx):
    return np.tile(idx.reshape(-1, 16).T, (8, 1)).astype(np.uint16)


def unstriped(offs):
    return offs[:16].T.reshape(-1).astype(np.int64)


def pack_weight(w):
    k, n = w.shape
    w = f64(np.asarray(w, np.float32).astype(ml_dtypes.bfloat16)).reshape(k // 32, 32, n)
    amax = np.abs(w).max(1)
    byte = np.clip(np.where(amax > 0, np.frexp(amax)[1] - 1 + 127 - 7, 1), 1, 254)
    scaled = (w * np.exp2(127.0 - byte)[:, None, :]).reshape(k, n).astype(np.float32)
    words = np.ascontiguousarray(scaled.reshape(k // 512, 128, 4, n).transpose(0, 1, 3, 2)).astype(ml_dtypes.float8_e4m3fn).view(np.uint8)
    return words, np.ascontiguousarray(byte.astype(np.uint8).reshape(k // 512, 16, n))


def unpack_weight(words, scales):
    g, p, n, _ = words.shape
    vals = np.ascontiguousarray(words).view(ml_dtypes.float8_e4m3fn).astype(np.float64) * np.repeat(np.exp2(scales.astype(np.float64) - 127.0), 8, axis=1)[..., None]
    return vals.transpose(0, 1, 3, 2).reshape(g * 512, n)


K, T, S, V = 512, 2048, 512, 256
P = 2 ** 7


def setup_inputs():
    n = np.random.standard_normal
    s = mx_kscale(K)[:, None]
    packed_xT = pack_weight(n((K, T)) * s)
    return {
        "x_words": packed_xT[0],
        "x_scales": packed_xT[1],
        "hT": (n((K, V)) / np.sqrt(K) / s).astype(np.float32),
        "inv": (np.tile(np.random.uniform(0.6, 1.4, T), (P, 1))).astype(np.float32),
        "isp": ((np.random.uniform(size=(V, S)) < 0.2) * 1.0).astype(np.float32),
        "offs": striped(np.random.permutation(T)[:S]),
    }


def reference(x_words, x_scales, hT, inv, isp, offs):
    hTq = mxq(f64(hT), 0, "e4m3")
    xq = unpack_weight(x_words, x_scales)[:, unstriped(offs)]
    y = (hTq.T @ xq) * (f64(inv)[:1][:, unstriped(offs)])
    en = (-1.0 * f64(isp) + 1.0) * (np.exp(1.5 * (y + 0.1)))
    tn = en.sum(axis=1, keepdims=True) + 1.0
    ep = f64(isp) * (np.exp(-1.5 * (y - 0.1)))
    tp = ep.sum(axis=1, keepdims=True) + 1.0
    return 50.0 * (en / tn - (ep / tp))

@@ -1,0 +1,158 @@
+from contextlib import ExitStack
+
+import concourse.mybir as mybir
+
+K, T, S, V = 512, 2048, 512, 256
+FLOPS = 2 * K * S * V
+
+F32 = mybir.dt.float32
+BF16 = mybir.dt.bfloat16
+I32 = mybir.dt.int32
+U32 = mybir.dt.uint32
+U16 = mybir.dt.uint16
+U8 = mybir.dt.uint8
+FP8X4 = mybir.dt.float8_e4m3fn_x4
+ALU = mybir.AluOpType
+ACT = mybir.ActivationFunctionType
+
+P = 128
+PACK = 4
+TILES = V // P
+HALVES = 2
+HALF = S // HALVES
+INV_ROW = 16
+
+
+def tile_picked_yprxan_grad_p_kernel(tc, x_words, x_scales, hT, inv, isp, offs, out):
+    nc = tc.nc
+    with ExitStack() as ctx:
+        sb = ctx.enter_context(tc.tile_pool(name="sb", bufs=1))
+        ps = ctx.enter_context(tc.psum_pool(name="ps", bufs=1))
+
+        offsets = sb.tile([P, S // 16], U16, name="offsets")
+        nc.sync.dma_start(offsets[:], offs)
+        half_offsets = [offsets[:, c * (HALF // 16) : (c + 1) * (HALF // 16)] for c in range(HALVES)]
+
+        isp_sb = [sb.tile([P, S], F32, name="isp0")]
+        nc.sync.dma_start(out=isp_sb[0][:], in_=isp[0:P, :])
+
+        scale_table = sb.tile([P, T], U8, name="scale_table", tag="scale_slot", align_bytes=64)
+        nc.gpsimd.memset(scale_table[:].bitcast(I32), 0)
+        for q in range(4):
+            nc.sync.dma_start(
+                out=scale_table[32 * q : 32 * q + 4, :].bitcast(I32),
+                in_=x_scales[0, 4 * q : 4 * q + 4, :].bitcast(I32),
+            )
+
+        zeros = sb.tile([P, P], F32, name="zeros", tag="h_slot")
+        nc.gpsimd.memset(zeros[:], 0.0)
+        ident = sb.tile([P, P], F32, name="ident")
+        nc.gpsimd.affine_select(
+            out=ident[:],
+            in_=zeros[:],
+            compare_op=ALU.not_equal,
+            fill=1.0,
+            base=0,
+            pattern=[[-1, P]],
+            channel_multiplier=1,
+        )
+        h_raw = sb.tile([P, PACK, V], F32, name="h_raw", tag="h_slot")
+        nc.sync.dma_start(out=h_raw[:], in_=hT.rearrange("(p j) w -> p j w", j=PACK))
+
+        inv_table = sb.tile([P, T], F32, name="inv_table", align_bytes=64)
+        nc.vector.memset(inv_table[:], 0.0)
+        nc.sync.dma_start(out=inv_table[INV_ROW : INV_ROW + 1, :], in_=inv[INV_ROW : INV_ROW + 1, :])
+
+        warm_in = sb.tile([P, 1], F32, name="warm_in", tag="word_slot", align_bytes=64)
+        warm_out = sb.tile([P, 1], F32, name="warm_out")
+        nc.vector.memset(warm_in[:], 0.0)
+        nc.scalar.activation(out=warm_out[:], in_=warm_in[:], func=ACT.Exp)
+
+        word_table = sb.tile([P, T], U32, name="word_table", tag="word_slot", align_bytes=64)
+        nc.sync.dma_start(
+            out=word_table[:].bitcast(I32), in_=x_words[0].rearrange("p n t -> p (n t)").bitcast(I32)
+        )
+
+        x_scale = sb.tile([P, S], U8, name="x_scale", align_bytes=64)
+        nc.vector.tensor_copy(x_scale[:], scale_table[:].indirect(offsets[:]))
+        isp_sb.append(sb.tile([P, S], F32, name="isp1", tag="scale_slot", align_bytes=64))
+        nc.sync.dma_start(out=isp_sb[1][:], in_=isp[P : 2 * P, :])
+
+        inv_wide = sb.tile([P, S], F32, name="inv_wide")
+        for c in range(HALVES):
+            picked = sb.tile([P, HALF], F32, name=f"inv_picked{c}")
+            nc.vector.tensor_copy(picked[:], inv_table[:].indirect(half_offsets[c]))
+            turned = ps.tile([P, 2, P], F32, name=f"inv_turned{c}")
+            for b in range(2):
+                nc.tensor.transpose(turned[:, b, :], picked[:, b * P : (b + 1) * P], ident[:])
+            column = sb.tile([P, 2], F32, name=f"inv_column{c}")
+            nc.scalar.copy(out=column[:], in_=turned[:, :, INV_ROW])
+            spread = ps.tile([P, 2, P], F32, name=f"inv_spread{c}")
+            for b in range(2):
+                nc.tensor.transpose(spread[:, b, :], column[:, b : b + 1].to_broadcast([P, P]), ident[:])
+            nc.scalar.copy(out=inv_wide[:, c * HALF : (c + 1) * HALF], in_=spread[:].rearrange("p b n -> p (b n)"))
+
+        h_codes, h_scale = [], []
+        for m in range(TILES):
+            grouped = sb.tile([P, P, PACK], BF16, name=f"h_grouped{m}", align_bytes=64)
+            nc.scalar.copy(out=grouped[:], in_=h_raw[:, :, m * P : (m + 1) * P].rearrange("p j w -> p w j"))
+            codes = sb.tile([P, P], U32, name=f"h_codes{m}", align_bytes=64)
+            scale = sb.tile([P, P], U8, name=f"h_scale{m}", align_bytes=64)
+            nc.vector.quantize_mx(
+                out=codes[:].bitcast(FP8X4), scales=scale[:], in_=grouped[:].rearrange("p w j -> p (w j)")
+            )
+            h_codes.append(codes)
+            h_scale.append(scale)
+
+        sims = [ps.tile([P, S], F32, name=f"sim{m}") for m in range(TILES)]
+        for c in range(HALVES):
+            cols = slice(c * HALF, (c + 1) * HALF)
+            x_codes = sb.tile([P, HALF], U32, name=f"x_codes{c}", align_bytes=64)
+            nc.vector.tensor_copy(x_codes[:], word_table[:].indirect(half_offsets[c]))
+            for m in range(TILES):
+                nc.tensor.matmul_mx(
+                    out=sims[m][:, cols],
+                    lhsT=h_codes[m][:].bitcast(FP8X4),
+                    lhsT_scale=h_scale[m][:],
+                    rhs=x_codes[:].bitcast(FP8X4),
+                    rhs_scale=x_scale[:, cols],
+                    start=True,
+                    stop=True,
+                )
+
+        pushes, pulls = [], []
+        for m in range(TILES):
+            y = sb.tile([P, S], F32, name=f"y{m}")
+            nc.vector.tensor_tensor(y[:], sims[m][:], inv_wide[:], ALU.mult)
+            push = sb.tile([P, S], F32, name=f"push{m}")
+            pull = sb.tile([P, S], F32, name=f"pull{m}")
+            nc.scalar.activation(out=push[:], in_=y[:], func=ACT.Exp, scale=1.5, bias=0.15)
+            nc.scalar.activation(out=pull[:], in_=y[:], func=ACT.Exp, scale=-1.5, bias=0.15)
+            pushes.append(push)
+            pulls.append(pull)
+
+        def weight(total, name):
+            denom = sb.tile([P, 1], F32, name=f"denom_{name}")
+            nc.scalar.activation(out=denom[:], in_=total[:], func=ACT.Identity, scale=-0.02, bias=0.02)
+            recip = sb.tile([P, 1], F32, name=f"recip_{name}")
+            nc.vector.reciprocal(recip[:], denom[:])
+            return recip
+
+        for m in range(TILES):
+            neg_en = sb.tile([P, S], F32, name=f"neg_en{m}")
+            neg_ep = sb.tile([P, S], F32, name=f"neg_ep{m}")
+            sum_n = sb.tile([P, 1], F32, name=f"sum_n{m}")
+            sum_p = sb.tile([P, 1], F32, name=f"sum_p{m}")
+            nc.vector.scalar_tensor_tensor(
+                neg_en[:], isp_sb[m][:], -1.0, pushes[m][:], ALU.add, ALU.mult, accum_out=sum_n[:]
+            )
+            nc.vector.scalar_tensor_tensor(
+                neg_ep[:], isp_sb[m][:], -1.0, pulls[m][:], ALU.mult, ALU.mult, accum_out=sum_p[:]
+            )
+            w_n = weight(sum_n, f"n{m}")
+            w_p = weight(sum_p, f"p{m}")
+            term_n = sb.tile([P, S], F32, name=f"term_n{m}")
+            nc.scalar.activation(out=term_n[:], in_=neg_en[:], func=ACT.Copy, scale=w_n[:])
+            res = sb.tile([P, S], F32, name=f"res{m}")
+            nc.vector.scalar_tensor_tensor(res[:], neg_ep[:], w_p[:], term_n[:], ALU.mult, ALU.subtract)
+            nc.sync.dma_start(out=out[m * P : (m + 1) * P, :], in_=res[:])

@@ -1,6 +1,7 @@
 from contextlib import ExitStack
 
 import concourse.mybir as mybir
+from concourse.masks import make_identity
 
 K, T, S, V = 512, 2048, 512, 256
 FLOPS = 2 * K * S * V
@@ -31,103 +32,100 @@ def tile_picked_yprxan_grad_p_kernel(tc, x_words, x_scales, hT, inv, isp, offs, 
 
         offsets = sb.tile([P, S // 16], U16, name="offsets")
         nc.sync.dma_start(offsets[:], offs)
-        half_offsets = [offsets[:, c * (HALF // 16) : (c + 1) * (HALF // 16)] for c in range(HALVES)]
 
-        isp_sb = [sb.tile([P, S], F32, name="isp0")]
-        nc.sync.dma_start(out=isp_sb[0][:], in_=isp[0:P, :])
+        inv_cols = sb.tile([P, 4, 8], F32, name="inv_cols", tag="grouped_slot", align_bytes=64)
+        nc.scalar.dma_start(out=inv_cols[:, :, 0:4], in_=inv[0].rearrange("(q p r) -> p q r", q=4, r=4))
 
         scale_table = sb.tile([P, T], U8, name="scale_table", tag="scale_slot", align_bytes=64)
-        nc.gpsimd.memset(scale_table[:].bitcast(I32), 0)
+        nc.vector.memset(scale_table[:].bitcast(I32), 0)
         for q in range(4):
-            nc.sync.dma_start(
+            (nc.sync if q < 2 else nc.scalar).dma_start(
                 out=scale_table[32 * q : 32 * q + 4, :].bitcast(I32),
                 in_=x_scales[0, 4 * q : 4 * q + 4, :].bitcast(I32),
             )
 
-        zeros = sb.tile([P, P], F32, name="zeros", tag="h_slot")
-        nc.gpsimd.memset(zeros[:], 0.0)
+        zero_col = sb.tile([P, 1], F32, name="zero_col", tag="word_slot", align_bytes=64)
+        nc.vector.memset(zero_col[:], 0.0)
+        margin = sb.tile([P, 1], F32, name="margin")
+        nc.vector.tensor_scalar_add(margin[:], zero_col[:], 0.15)
         ident = sb.tile([P, P], F32, name="ident")
-        nc.gpsimd.affine_select(
-            out=ident[:],
-            in_=zeros[:],
-            compare_op=ALU.not_equal,
-            fill=1.0,
-            base=0,
-            pattern=[[-1, P]],
-            channel_multiplier=1,
-        )
-        h_raw = sb.tile([P, PACK, V], F32, name="h_raw", tag="h_slot")
-        nc.sync.dma_start(out=h_raw[:], in_=hT.rearrange("(p j) w -> p j w", j=PACK))
-
-        inv_table = sb.tile([P, T], F32, name="inv_table", align_bytes=64)
-        nc.vector.memset(inv_table[:], 0.0)
-        nc.sync.dma_start(out=inv_table[INV_ROW : INV_ROW + 1, :], in_=inv[INV_ROW : INV_ROW + 1, :])
-
-        warm_in = sb.tile([P, 1], F32, name="warm_in", tag="word_slot", align_bytes=64)
-        warm_out = sb.tile([P, 1], F32, name="warm_out")
-        nc.vector.memset(warm_in[:], 0.0)
-        nc.scalar.activation(out=warm_out[:], in_=warm_in[:], func=ACT.Exp)
-
+        make_identity(nc, ident[:])
         word_table = sb.tile([P, T], U32, name="word_table", tag="word_slot", align_bytes=64)
         nc.sync.dma_start(
             out=word_table[:].bitcast(I32), in_=x_words[0].rearrange("p n t -> p (n t)").bitcast(I32)
         )
 
+        warm_in = sb.tile([P, 1], F32, name="warm_in", tag="h_slot0")
+        warm_out = sb.tile([P, 1], F32, name="warm_out", tag="h_slot1")
+        nc.vector.memset(warm_in[:], 0.0)
+        nc.scalar.activation(out=warm_out[:], in_=warm_in[:], func=ACT.Exp)
+        h_raw = []
+        for m in range(TILES):
+            h_raw.append(sb.tile([P, PACK, P], F32, name=f"h_raw{m}", tag=f"h_slot{m}"))
+            nc.sync.dma_start(
+                out=h_raw[m][:], in_=hT[:, m * P : (m + 1) * P].rearrange("(p j) w -> p j w", j=PACK)
+            )
+
+        inv_table = sb.tile([P, T], F32, name="inv_table", align_bytes=64)
+        for q in range(4):
+            spread = ps.tile([P, 4, P], F32, name=f"inv_spread{q}")
+            for r in range(4):
+                nc.tensor.transpose(spread[:, r, :], inv_cols[:, q, r : r + 1].to_broadcast([P, P]), ident[:])
+            nc.scalar.copy(
+                out=inv_table[:, q * 512 : (q + 1) * 512].rearrange("p (n r) -> p n r", r=4),
+                in_=spread[:].rearrange("p r n -> p n r"),
+            )
+
         x_scale = sb.tile([P, S], U8, name="x_scale", align_bytes=64)
         nc.vector.tensor_copy(x_scale[:], scale_table[:].indirect(offsets[:]))
-        isp_sb.append(sb.tile([P, S], F32, name="isp1", tag="scale_slot", align_bytes=64))
-        nc.sync.dma_start(out=isp_sb[1][:], in_=isp[P : 2 * P, :])
+        isp_sb = sb.tile([P, TILES, S], F32, name="isp_sb", tag="scale_slot", align_bytes=64)
+        nc.sync.dma_start(out=isp_sb[:], in_=isp.rearrange("(m p) s -> p m s", p=P))
 
-        inv_wide = sb.tile([P, S], F32, name="inv_wide")
-        for c in range(HALVES):
-            picked = sb.tile([P, HALF], F32, name=f"inv_picked{c}")
-            nc.vector.tensor_copy(picked[:], inv_table[:].indirect(half_offsets[c]))
-            turned = ps.tile([P, 2, P], F32, name=f"inv_turned{c}")
-            for b in range(2):
-                nc.tensor.transpose(turned[:, b, :], picked[:, b * P : (b + 1) * P], ident[:])
-            column = sb.tile([P, 2], F32, name=f"inv_column{c}")
-            nc.scalar.copy(out=column[:], in_=turned[:, :, INV_ROW])
-            spread = ps.tile([P, 2, P], F32, name=f"inv_spread{c}")
-            for b in range(2):
-                nc.tensor.transpose(spread[:, b, :], column[:, b : b + 1].to_broadcast([P, P]), ident[:])
-            nc.scalar.copy(out=inv_wide[:, c * HALF : (c + 1) * HALF], in_=spread[:].rearrange("p b n -> p (b n)"))
+        x_codes = sb.tile([P, S], U32, name="x_codes", align_bytes=64)
+        nc.vector.tensor_copy(x_codes[:], word_table[:].indirect(offsets[:]))
 
         h_codes, h_scale = [], []
+        grouped = sb.tile([P, TILES, P, PACK], BF16, name="h_grouped", tag="grouped_slot", align_bytes=64)
         for m in range(TILES):
-            grouped = sb.tile([P, P, PACK], BF16, name=f"h_grouped{m}", align_bytes=64)
-            nc.scalar.copy(out=grouped[:], in_=h_raw[:, :, m * P : (m + 1) * P].rearrange("p j w -> p w j"))
+            nc.scalar.copy(out=grouped[:, m], in_=h_raw[m][:].rearrange("p j w -> p w j"))
             codes = sb.tile([P, P], U32, name=f"h_codes{m}", align_bytes=64)
             scale = sb.tile([P, P], U8, name=f"h_scale{m}", align_bytes=64)
             nc.vector.quantize_mx(
-                out=codes[:].bitcast(FP8X4), scales=scale[:], in_=grouped[:].rearrange("p w j -> p (w j)")
+                out=codes[:].bitcast(FP8X4), scales=scale[:], in_=grouped[:, m].rearrange("p w j -> p (w j)")
             )
             h_codes.append(codes)
             h_scale.append(scale)
 
-        sims = [ps.tile([P, S], F32, name=f"sim{m}") for m in range(TILES)]
+        inv_picked = []
         for c in range(HALVES):
-            cols = slice(c * HALF, (c + 1) * HALF)
-            x_codes = sb.tile([P, HALF], U32, name=f"x_codes{c}", align_bytes=64)
-            nc.vector.tensor_copy(x_codes[:], word_table[:].indirect(half_offsets[c]))
-            for m in range(TILES):
-                nc.tensor.matmul_mx(
-                    out=sims[m][:, cols],
-                    lhsT=h_codes[m][:].bitcast(FP8X4),
-                    lhsT_scale=h_scale[m][:],
-                    rhs=x_codes[:].bitcast(FP8X4),
-                    rhs_scale=x_scale[:, cols],
-                    start=True,
-                    stop=True,
-                )
+            picked = sb.tile([P, HALF], F32, name=f"inv_picked{c}", tag="inv_first" if c == 0 else "h_slot0")
+            nc.vector.tensor_copy(
+                picked[:], inv_table[:].indirect(offsets[:, c * (HALF // 16) : (c + 1) * (HALF // 16)])
+            )
+            inv_picked.append(picked)
+
+        sims = [ps.tile([P, S], F32, name=f"sim{m}") for m in range(TILES)]
+        for m in range(TILES):
+            nc.tensor.matmul_mx(
+                out=sims[m][:],
+                lhsT=h_codes[m][:].bitcast(FP8X4),
+                lhsT_scale=h_scale[m][:],
+                rhs=x_codes[:].bitcast(FP8X4),
+                rhs_scale=x_scale[:],
+                start=True,
+                stop=True,
+            )
 
         pushes, pulls = [], []
         for m in range(TILES):
-            y = sb.tile([P, S], F32, name=f"y{m}")
-            nc.vector.tensor_tensor(y[:], sims[m][:], inv_wide[:], ALU.mult)
+            y = sb.tile([P, S], F32, name=f"y{m}", tag="h_slot1" if m == 0 else "y1")
+            for c in range(HALVES):
+                cols = slice(c * HALF, (c + 1) * HALF)
+                nc.vector.tensor_tensor(y[:, cols], sims[m][:, cols], inv_picked[c][:], ALU.mult)
             push = sb.tile([P, S], F32, name=f"push{m}")
             pull = sb.tile([P, S], F32, name=f"pull{m}")
-            nc.scalar.activation(out=push[:], in_=y[:], func=ACT.Exp, scale=1.5, bias=0.15)
-            nc.scalar.activation(out=pull[:], in_=y[:], func=ACT.Exp, scale=-1.5, bias=0.15)
+            nc.scalar.activation(out=push[:], in_=y[:], func=ACT.Exp, scale=1.5, bias=margin[:])
+            nc.scalar.activation(out=pull[:], in_=y[:], func=ACT.Exp, scale=-1.5, bias=margin[:])
             pushes.append(push)
             pulls.append(pull)
 
@@ -144,15 +142,20 @@ def tile_picked_yprxan_grad_p_kernel(tc, x_words, x_scales, hT, inv, isp, offs, 
             sum_n = sb.tile([P, 1], F32, name=f"sum_n{m}")
             sum_p = sb.tile([P, 1], F32, name=f"sum_p{m}")
             nc.vector.scalar_tensor_tensor(
-                neg_en[:], isp_sb[m][:], -1.0, pushes[m][:], ALU.add, ALU.mult, accum_out=sum_n[:]
+                neg_en[:], isp_sb[:, m, :], -1.0, pushes[m][:], ALU.add, ALU.mult, accum_out=sum_n[:]
             )
             nc.vector.scalar_tensor_tensor(
-                neg_ep[:], isp_sb[m][:], -1.0, pulls[m][:], ALU.mult, ALU.mult, accum_out=sum_p[:]
+                neg_ep[:], isp_sb[:, m, :], -1.0, pulls[m][:], ALU.mult, ALU.mult, accum_out=sum_p[:]
             )
             w_n = weight(sum_n, f"n{m}")
             w_p = weight(sum_p, f"p{m}")
             term_n = sb.tile([P, S], F32, name=f"term_n{m}")
             nc.scalar.activation(out=term_n[:], in_=neg_en[:], func=ACT.Copy, scale=w_n[:])
             res = sb.tile([P, S], F32, name=f"res{m}")
-            nc.vector.scalar_tensor_tensor(res[:], neg_ep[:], w_p[:], term_n[:], ALU.mult, ALU.subtract)
-            nc.sync.dma_start(out=out[m * P : (m + 1) * P, :], in_=res[:])
+            pieces = 1 if m == 0 else 2
+            for c in range(pieces):
+                cols = slice(c * S // pieces, (c + 1) * S // pieces)
+                nc.vector.scalar_tensor_tensor(
+                    res[:, cols], neg_ep[:, cols], w_p[:], term_n[:, cols], ALU.mult, ALU.subtract
+                )
+                nc.sync.dma_start(out=out[m * P : (m + 1) * P, cols], in_=res[:, cols])

@@ -33,51 +33,48 @@ def tile_picked_yprxan_grad_p_kernel(tc, x_words, x_scales, hT, inv, isp, offs, 
         offsets = sb.tile([P, S // 16], U16, name="offsets")
         nc.sync.dma_start(offsets[:], offs)
 
-        inv_cols = sb.tile([P, 4, 8], F32, name="inv_cols", tag="grouped_slot", align_bytes=64)
-        nc.scalar.dma_start(out=inv_cols[:, :, 0:4], in_=inv[0].rearrange("(q p r) -> p q r", q=4, r=4))
-
-        scale_table = sb.tile([P, T], U8, name="scale_table", tag="scale_slot", align_bytes=64)
-        nc.vector.memset(scale_table[:].bitcast(I32), 0)
-        for q in range(4):
-            (nc.sync if q < 2 else nc.scalar).dma_start(
-                out=scale_table[32 * q : 32 * q + 4, :].bitcast(I32),
-                in_=x_scales[0, 4 * q : 4 * q + 4, :].bitcast(I32),
-            )
+        inv_cols = sb.tile([P, T // P], F32, name="inv_cols", tag="grouped0", align_bytes=64)
+        nc.sync.dma_start(out=inv_cols[:], in_=inv[0].rearrange("(p b) -> p b", p=P))
 
         zero_col = sb.tile([P, 1], F32, name="zero_col", tag="word_slot", align_bytes=64)
         nc.vector.memset(zero_col[:], 0.0)
+        scale_table = sb.tile([P, T], U8, name="scale_table", tag="scale_slot", align_bytes=64)
+        nc.vector.memset(scale_table[:].bitcast(I32), 0)
+        nc.sync.dma_start(out=scale_table[0:P:8, :].bitcast(I32), in_=x_scales[0].bitcast(I32))
         margin = sb.tile([P, 1], F32, name="margin")
         nc.vector.tensor_scalar_add(margin[:], zero_col[:], 0.15)
-        ident = sb.tile([P, P], F32, name="ident")
-        make_identity(nc, ident[:])
         word_table = sb.tile([P, T], U32, name="word_table", tag="word_slot", align_bytes=64)
         nc.sync.dma_start(
             out=word_table[:].bitcast(I32), in_=x_words[0].rearrange("p n t -> p (n t)").bitcast(I32)
         )
+        x_scale = sb.tile([P, S], U8, name="x_scale", align_bytes=64)
+        nc.vector.memset(x_scale[:].bitcast(I32), 0)
 
-        warm_in = sb.tile([P, 1], F32, name="warm_in", tag="h_slot0")
-        warm_out = sb.tile([P, 1], F32, name="warm_out", tag="h_slot1")
-        nc.vector.memset(warm_in[:], 0.0)
-        nc.scalar.activation(out=warm_out[:], in_=warm_in[:], func=ACT.Exp)
-        h_raw = []
-        for m in range(TILES):
-            h_raw.append(sb.tile([P, PACK, P], F32, name=f"h_raw{m}", tag=f"h_slot{m}"))
-            nc.sync.dma_start(
-                out=h_raw[m][:], in_=hT[:, m * P : (m + 1) * P].rearrange("(p j) w -> p j w", j=PACK)
-            )
+        ident = sb.tile([P, P], F32, name="ident", tag="grouped1", align_bytes=64)
+        make_identity(nc, ident[:])
+
+        warm_out = sb.tile([P, 1], F32, name="warm_out", tag="h_slot")
+        nc.scalar.activation(out=warm_out[:], in_=margin[:], func=ACT.Exp)
+        h_raw = sb.tile([P, PACK, V], F32, name="h_raw", tag="h_slot")
+        nc.sync.dma_start(out=h_raw[:], in_=hT.rearrange("(p j) w -> p j w", j=PACK))
+
 
         inv_table = sb.tile([P, T], F32, name="inv_table", align_bytes=64)
         for q in range(4):
             spread = ps.tile([P, 4, P], F32, name=f"inv_spread{q}")
             for r in range(4):
-                nc.tensor.transpose(spread[:, r, :], inv_cols[:, q, r : r + 1].to_broadcast([P, P]), ident[:])
+                nc.tensor.transpose(spread[:, r, :], inv_cols[:, 4 * q + r : 4 * q + r + 1].to_broadcast([P, P]), ident[:])
             nc.scalar.copy(
-                out=inv_table[:, q * 512 : (q + 1) * 512].rearrange("p (n r) -> p n r", r=4),
+                out=inv_table[:].rearrange("p (n b) -> p n b", n=P)[:, :, 4 * q : 4 * q + 4],
                 in_=spread[:].rearrange("p r n -> p n r"),
             )
 
-        x_scale = sb.tile([P, S], U8, name="x_scale", align_bytes=64)
-        nc.vector.tensor_copy(x_scale[:], scale_table[:].indirect(offsets[:]))
+        picked_scale = sb.tile([P, S], U8, name="picked_scale", align_bytes=64)
+        nc.vector.tensor_copy(picked_scale[:], scale_table[:].indirect(offsets[:]))
+        for r in range(4):
+            nc.sync.dma_start(
+                out=x_scale[r:P:32, :].bitcast(I32), in_=picked_scale[8 * r : P : 32, :].bitcast(I32)
+            )
         isp_sb = sb.tile([P, TILES, S], F32, name="isp_sb", tag="scale_slot", align_bytes=64)
         nc.sync.dma_start(out=isp_sb[:], in_=isp.rearrange("(m p) s -> p m s", p=P))
 
@@ -85,43 +82,48 @@ def tile_picked_yprxan_grad_p_kernel(tc, x_words, x_scales, hT, inv, isp, offs, 
         nc.vector.tensor_copy(x_codes[:], word_table[:].indirect(offsets[:]))
 
         h_codes, h_scale = [], []
-        grouped = sb.tile([P, TILES, P, PACK], BF16, name="h_grouped", tag="grouped_slot", align_bytes=64)
         for m in range(TILES):
-            nc.scalar.copy(out=grouped[:, m], in_=h_raw[m][:].rearrange("p j w -> p w j"))
+            grouped = sb.tile([P, P, PACK], BF16, name=f"h_grouped{m}", tag=f"grouped{m}", align_bytes=64)
+            nc.scalar.copy(
+                out=grouped[:].rearrange("p (c i) j -> p c j i", i=4),
+                in_=h_raw[:, :, m * P : (m + 1) * P].rearrange("p j (c i) -> p c j i", i=4),
+            )
             codes = sb.tile([P, P], U32, name=f"h_codes{m}", align_bytes=64)
             scale = sb.tile([P, P], U8, name=f"h_scale{m}", align_bytes=64)
             nc.vector.quantize_mx(
-                out=codes[:].bitcast(FP8X4), scales=scale[:], in_=grouped[:, m].rearrange("p w j -> p (w j)")
+                out=codes[:].bitcast(FP8X4), scales=scale[:], in_=grouped[:].rearrange("p w j -> p (w j)")
             )
             h_codes.append(codes)
             h_scale.append(scale)
 
         inv_picked = []
         for c in range(HALVES):
-            picked = sb.tile([P, HALF], F32, name=f"inv_picked{c}", tag="inv_first" if c == 0 else "h_slot0")
+            picked = sb.tile([P, HALF], F32, name=f"inv_picked{c}", tag="inv_first" if c == 0 else "grouped0", align_bytes=64)
             nc.vector.tensor_copy(
                 picked[:], inv_table[:].indirect(offsets[:, c * (HALF // 16) : (c + 1) * (HALF // 16)])
             )
             inv_picked.append(picked)
 
-        sims = [ps.tile([P, S], F32, name=f"sim{m}") for m in range(TILES)]
+        sims = [[ps.tile([P, HALF], F32, name=f"sim{m}_{c}") for c in range(HALVES)] for m in range(TILES)]
         for m in range(TILES):
-            nc.tensor.matmul_mx(
-                out=sims[m][:],
-                lhsT=h_codes[m][:].bitcast(FP8X4),
-                lhsT_scale=h_scale[m][:],
-                rhs=x_codes[:].bitcast(FP8X4),
-                rhs_scale=x_scale[:],
-                start=True,
-                stop=True,
-            )
+            for c in range(HALVES):
+                cols = slice(c * HALF, (c + 1) * HALF)
+                nc.tensor.matmul_mx(
+                    out=sims[m][c][:],
+                    lhsT=h_codes[m][:].bitcast(FP8X4),
+                    lhsT_scale=h_scale[m][:],
+                    rhs=x_codes[:, cols].bitcast(FP8X4),
+                    rhs_scale=x_scale[:, cols],
+                    start=True,
+                    stop=True,
+                )
 
         pushes, pulls = [], []
         for m in range(TILES):
-            y = sb.tile([P, S], F32, name=f"y{m}", tag="h_slot1" if m == 0 else "y1")
+            y = sb.tile([P, S], F32, name=f"y{m}", tag="h_slot" if m == 0 else "y1")
             for c in range(HALVES):
                 cols = slice(c * HALF, (c + 1) * HALF)
-                nc.vector.tensor_tensor(y[:, cols], sims[m][:, cols], inv_picked[c][:], ALU.mult)
+                nc.vector.tensor_tensor(y[:, cols], sims[m][c][:], inv_picked[c][:], ALU.mult)
             push = sb.tile([P, S], F32, name=f"push{m}")
             pull = sb.tile([P, S], F32, name=f"pull{m}")
             nc.scalar.activation(out=push[:], in_=y[:], func=ACT.Exp, scale=1.5, bias=margin[:])

@@ -118,6 +118,7 @@ def tile_picked_yprxan_grad_p_kernel(tc, x_words, x_scales, hT, inv, isp, offs, 
                     stop=True,
                 )
 
+        halves = [slice(c * HALF, (c + 1) * HALF) for c in range(HALVES)]
         pushes, pulls = [], []
         for m in range(TILES):
             y = sb.tile([P, S], F32, name=f"y{m}", tag="h_slot" if m == 0 else "y1")
@@ -126,7 +127,8 @@ def tile_picked_yprxan_grad_p_kernel(tc, x_words, x_scales, hT, inv, isp, offs, 
                 nc.vector.tensor_tensor(y[:, cols], sims[m][c][:], inv_picked[c][:], ALU.mult)
             push = sb.tile([P, S], F32, name=f"push{m}")
             pull = sb.tile([P, S], F32, name=f"pull{m}")
-            nc.scalar.activation(out=push[:], in_=y[:], func=ACT.Exp, scale=1.5, bias=margin[:])
+            for cols in halves if m == 0 else [slice(0, S)]:
+                nc.scalar.activation(out=push[:, cols], in_=y[:, cols], func=ACT.Exp, scale=1.5, bias=margin[:])
             nc.scalar.activation(out=pull[:], in_=y[:], func=ACT.Exp, scale=-1.5, bias=margin[:])
             pushes.append(push)
             pulls.append(pull)
@@ -152,11 +154,9 @@ def tile_picked_yprxan_grad_p_kernel(tc, x_words, x_scales, hT, inv, isp, offs, 
             w_n = weight(sum_n, f"n{m}")
             w_p = weight(sum_p, f"p{m}")
             term_n = sb.tile([P, S], F32, name=f"term_n{m}")
-            nc.scalar.activation(out=term_n[:], in_=neg_en[:], func=ACT.Copy, scale=w_n[:])
             res = sb.tile([P, S], F32, name=f"res{m}")
-            pieces = 1 if m == 0 else 2
-            for c in range(pieces):
-                cols = slice(c * S // pieces, (c + 1) * S // pieces)
+            for cols in halves:
+                nc.scalar.activation(out=term_n[:, cols], in_=neg_en[:, cols], func=ACT.Copy, scale=w_n[:])
                 nc.vector.scalar_tensor_tensor(
                     res[:, cols], neg_ep[:, cols], w_p[:], term_n[:, cols], ALU.mult, ALU.subtract
                 )

from contextlib import ExitStack

import concourse.mybir as mybir
from concourse.masks import make_identity

K, T, S, V = 512, 2048, 512, 256
FLOPS = 2 * K * S * V

F32 = mybir.dt.float32
BF16 = mybir.dt.bfloat16
I32 = mybir.dt.int32
U32 = mybir.dt.uint32
U16 = mybir.dt.uint16
U8 = mybir.dt.uint8
FP8X4 = mybir.dt.float8_e4m3fn_x4
ALU = mybir.AluOpType
ACT = mybir.ActivationFunctionType

P = 128
PACK = 4
TILES = V // P
HALVES = 2
HALF = S // HALVES
INV_ROW = 16


def tile_picked_yprxan_grad_p_kernel(tc, x_words, x_scales, hT, inv, isp, offs, out):
    nc = tc.nc
    with ExitStack() as ctx:
        sb = ctx.enter_context(tc.tile_pool(name="sb", bufs=1))
        ps = ctx.enter_context(tc.psum_pool(name="ps", bufs=1))

        offsets = sb.tile([P, S // 16], U16, name="offsets")
        nc.sync.dma_start(offsets[:], offs)

        inv_cols = sb.tile([P, T // P], F32, name="inv_cols", tag="grouped0", align_bytes=64)
        nc.sync.dma_start(out=inv_cols[:], in_=inv[0].rearrange("(p b) -> p b", p=P))

        zero_col = sb.tile([P, 1], F32, name="zero_col", tag="word_slot", align_bytes=64)
        nc.vector.memset(zero_col[:], 0.0)
        scale_table = sb.tile([P, T], U8, name="scale_table", tag="scale_slot", align_bytes=64)
        nc.vector.memset(scale_table[:].bitcast(I32), 0)
        nc.sync.dma_start(out=scale_table[0:P:8, :].bitcast(I32), in_=x_scales[0].bitcast(I32))
        margin = sb.tile([P, 1], F32, name="margin")
        nc.vector.tensor_scalar_add(margin[:], zero_col[:], 0.15)
        word_table = sb.tile([P, T], U32, name="word_table", tag="word_slot", align_bytes=64)
        nc.sync.dma_start(
            out=word_table[:].bitcast(I32), in_=x_words[0].rearrange("p n t -> p (n t)").bitcast(I32)
        )
        x_scale = sb.tile([P, S], U8, name="x_scale", align_bytes=64)
        nc.vector.memset(x_scale[:].bitcast(I32), 0)

        ident = sb.tile([P, P], F32, name="ident", tag="grouped1", align_bytes=64)
        make_identity(nc, ident[:])

        warm_out = sb.tile([P, 1], F32, name="warm_out", tag="h_slot")
        nc.scalar.activation(out=warm_out[:], in_=margin[:], func=ACT.Exp)
        h_raw = sb.tile([P, PACK, V], F32, name="h_raw", tag="h_slot")
        nc.sync.dma_start(out=h_raw[:], in_=hT.rearrange("(p j) w -> p j w", j=PACK))


        inv_table = sb.tile([P, T], F32, name="inv_table", align_bytes=64)
        for q in range(4):
            spread = ps.tile([P, 4, P], F32, name=f"inv_spread{q}")
            for r in range(4):
                nc.tensor.transpose(spread[:, r, :], inv_cols[:, 4 * q + r : 4 * q + r + 1].to_broadcast([P, P]), ident[:])
            nc.scalar.copy(
                out=inv_table[:].rearrange("p (n b) -> p n b", n=P)[:, :, 4 * q : 4 * q + 4],
                in_=spread[:].rearrange("p r n -> p n r"),
            )

        picked_scale = sb.tile([P, S], U8, name="picked_scale", align_bytes=64)
        nc.vector.tensor_copy(picked_scale[:], scale_table[:].indirect(offsets[:]))
        for r in range(4):
            nc.sync.dma_start(
                out=x_scale[r:P:32, :].bitcast(I32), in_=picked_scale[8 * r : P : 32, :].bitcast(I32)
            )
        isp_sb = sb.tile([P, TILES, S], F32, name="isp_sb", tag="scale_slot", align_bytes=64)
        nc.sync.dma_start(out=isp_sb[:], in_=isp.rearrange("(m p) s -> p m s", p=P))

        x_codes = sb.tile([P, S], U32, name="x_codes", align_bytes=64)
        nc.vector.tensor_copy(x_codes[:], word_table[:].indirect(offsets[:]))

        h_codes, h_scale = [], []
        for m in range(TILES):
            grouped = sb.tile([P, P, PACK], BF16, name=f"h_grouped{m}", tag=f"grouped{m}", align_bytes=64)
            nc.scalar.copy(
                out=grouped[:].rearrange("p (c i) j -> p c j i", i=4),
                in_=h_raw[:, :, m * P : (m + 1) * P].rearrange("p j (c i) -> p c j i", i=4),
            )
            codes = sb.tile([P, P], U32, name=f"h_codes{m}", align_bytes=64)
            scale = sb.tile([P, P], U8, name=f"h_scale{m}", align_bytes=64)
            nc.vector.quantize_mx(
                out=codes[:].bitcast(FP8X4), scales=scale[:], in_=grouped[:].rearrange("p w j -> p (w j)")
            )
            h_codes.append(codes)
            h_scale.append(scale)

        inv_picked = []
        for c in range(HALVES):
            picked = sb.tile([P, HALF], F32, name=f"inv_picked{c}", tag="inv_first" if c == 0 else "grouped0", align_bytes=64)
            nc.vector.tensor_copy(
                picked[:], inv_table[:].indirect(offsets[:, c * (HALF // 16) : (c + 1) * (HALF // 16)])
            )
            inv_picked.append(picked)

        sims = [[ps.tile([P, HALF], F32, name=f"sim{m}_{c}") for c in range(HALVES)] for m in range(TILES)]
        for m in range(TILES):
            for c in range(HALVES):
                cols = slice(c * HALF, (c + 1) * HALF)
                nc.tensor.matmul_mx(
                    out=sims[m][c][:],
                    lhsT=h_codes[m][:].bitcast(FP8X4),
                    lhsT_scale=h_scale[m][:],
                    rhs=x_codes[:, cols].bitcast(FP8X4),
                    rhs_scale=x_scale[:, cols],
                    start=True,
                    stop=True,
                )

        halves = [slice(c * HALF, (c + 1) * HALF) for c in range(HALVES)]
        pushes, pulls = [], []
        for m in range(TILES):
            y = sb.tile([P, S], F32, name=f"y{m}", tag="h_slot" if m == 0 else "y1")
            for c in range(HALVES):
                cols = slice(c * HALF, (c + 1) * HALF)
                nc.vector.tensor_tensor(y[:, cols], sims[m][c][:], inv_picked[c][:], ALU.mult)
            push = sb.tile([P, S], F32, name=f"push{m}")
            pull = sb.tile([P, S], F32, name=f"pull{m}")
            for cols in halves if m == 0 else [slice(0, S)]:
                nc.scalar.activation(out=push[:, cols], in_=y[:, cols], func=ACT.Exp, scale=1.5, bias=margin[:])
            nc.scalar.activation(out=pull[:], in_=y[:], func=ACT.Exp, scale=-1.5, bias=margin[:])
            pushes.append(push)
            pulls.append(pull)

        def weight(total, name):
            denom = sb.tile([P, 1], F32, name=f"denom_{name}")
            nc.scalar.activation(out=denom[:], in_=total[:], func=ACT.Identity, scale=-0.02, bias=0.02)
            recip = sb.tile([P, 1], F32, name=f"recip_{name}")
            nc.vector.reciprocal(recip[:], denom[:])
            return recip

        for m in range(TILES):
            neg_en = sb.tile([P, S], F32, name=f"neg_en{m}")
            neg_ep = sb.tile([P, S], F32, name=f"neg_ep{m}")
            sum_n = sb.tile([P, 1], F32, name=f"sum_n{m}")
            sum_p = sb.tile([P, 1], F32, name=f"sum_p{m}")
            nc.vector.scalar_tensor_tensor(
                neg_en[:], isp_sb[:, m, :], -1.0, pushes[m][:], ALU.add, ALU.mult, accum_out=sum_n[:]
            )
            nc.vector.scalar_tensor_tensor(
                neg_ep[:], isp_sb[:, m, :], -1.0, pulls[m][:], ALU.mult, ALU.mult, accum_out=sum_p[:]
            )
            w_n = weight(sum_n, f"n{m}")
            w_p = weight(sum_p, f"p{m}")
            term_n = sb.tile([P, S], F32, name=f"term_n{m}")
            res = sb.tile([P, S], F32, name=f"res{m}")
            for cols in halves:
                nc.scalar.activation(out=term_n[:, cols], in_=neg_en[:, cols], func=ACT.Copy, scale=w_n[:])
                nc.vector.scalar_tensor_tensor(
                    res[:, cols], neg_ep[:, cols], w_p[:], term_n[:, cols], ALU.mult, ALU.subtract
                )
                nc.sync.dma_start(out=out[m * P : (m + 1) * P, cols], in_=res[:, cols])
